import numpy as np
CORES = [8,9,10,11,12,13,14,15,16,17,18,19,20,21,22,23]
N = 16
ROOT = 10
def setup_inputs(rng):
    return {"x": rng.standard_normal((N, 128, 4), dtype=np.float32)}
def reference(x):
    y = np.full(x.shape, np.nan, x.dtype)
    y[ROOT] = x.sum(axis=0, dtype=np.float64).astype(x.dtype)
    return {"y": y}

from concourse.bass import DstId, RemoteDMATransfer
from concourse.mybir import AluOpType

SCRATCH = {
    "stage": ("dram", [128, 4], "float32"),
    "slots": ("dram", [8, 128, 4], "float32"),
    "part_far": ("dram", [128, 4], "float32"),
    "part_near": ("dram", [128, 4], "float32"),
}
SEMAPHORES = ["loaded", "sent", "arrived", "far", "near", "copied", "stored"]

ROOT_COLLECTOR = 19
FAR_COLLECTOR = 10
ENG = 4
MASK = 0x000F


def rank_program(g, core, T, topo):
    if T.rank_of(core) is None:
        return
    root = T.cores[T.root]
    collector = ROOT_COLLECTOR if topo.chip(core) == topo.chip(root) else FAR_COLLECTOR
    k = core % 8

    if core == collector:
        g.sync.dma_start(T.slots[k], T.x[:]).then_inc(T.sem.loaded, 16)
        g.wait_ge(T.sem.loaded, 16)
        g.wait_ge(T.sem.arrived, 7 * ENG)
        rid, pid, _se = topo.addr(root)
        far = topo.chip(core) != topo.chip(root)
        g.remote_dma_fused(
            [RemoteDMATransfer(
                dst_ids=[DstId(rid=rid, pnc=pid)],
                dma_engine_mask=MASK,
                remote_sem=T.sem.far if far else T.sem.near,
                srcs=[T.slots[j] for j in range(8)],
                dsts=[T.part_far[:] if far else T.part_near[:]],
                alu_op=1,
            )],
            local_sem=T.sem.sent,
        )
        g.wait_ge(T.sem.sent, ENG)
        return

    g.sync.dma_start(T.stage[:], T.x[:]).then_inc(T.sem.loaded, 16)
    g.wait_ge(T.sem.loaded, 16)
    rid, pid, _se = topo.addr(collector)
    g.remote_dma(T.slots[k], T.stage[:], T.sem.arrived, T.sem.sent, pid, rid, MASK)
    g.wait_ge(T.sem.sent, ENG)

    if core == root:
        g.sync.wait_ge(T.sem.near, ENG)
        g.sync.dma_start(T.y[:], T.part_near[:]).then_inc(T.sem.copied, 16)
        g.wait_ge(T.sem.copied, 16)
        g.wait_ge(T.sem.far, ENG)
        g.dma_start(T.y[:], T.part_far[:], accum_op=AluOpType.add).then_inc(T.sem.stored, 16)
        g.wait_ge(T.sem.stored, 16)
